import numpy as np
import ml_dtypes


def mxq(x, axis, fmt="e4m3"):
    dtype, down = {"e4m3": (ml_dtypes.float8_e4m3fn, 7), "e5m2": (ml_dtypes.float8_e5m2, 14)}[fmt]
    v = np.moveaxis(np.asarray(x, np.float32).astype(ml_dtypes.bfloat16).astype(np.float64), axis, -1)
    blocks = v.reshape(v.shape[:-1] + (-1, 32))
    amax = np.abs(blocks).max(-1, keepdims=True)
    byte = np.maximum(np.where(amax > 0, np.frexp(amax)[1] - 1 + 127, 0) - down, 1)
    scale = np.exp2(byte - 127.0)
    codes = (blocks / scale).astype(np.float32).astype(dtype).astype(np.float64)
    return np.moveaxis((codes * scale).reshape(v.shape), -1, axis)


WIDE = False


def mx_kscale(k, group=512):
    if not WIDE:
        return np.ones(k)
    levels = np.array([10, -10, 5, -5, 0])
    if group != 512:
        return np.exp2(np.random.permutation(np.resize(levels, k // group))).repeat(group)
    if k % 512:
        return np.exp2(np.random.permutation(np.resize(levels, k // 32))).repeat(32)
    a = np.empty((k // 512, 16))
    for p in range(k // 512):
        a[p, :8] = np.random.permutation(np.resize(levels, 8))
        for g in range(8):
            far = levels[np.abs(levels - a[p, g]) >= 10]
            a[p, g + 8] = far[np.random.randint(len(far))]
    return np.exp2(a.ravel()).repeat(32)


def f64(x):
    return np.asarray(x).astype(np.float64)


def striped(idx):
    return np.tile(np.asarray(idx).reshape(-1, 16).T, (8, 1)).astype(np.uint16)


def unstriped(offs):
    return offs[:16].T.reshape(-1).astype(np.int64)


H, KV, D, NQ, N = 8, 2, 128, 512, 512


def setup_inputs():
    n = np.random.standard_normal
    s = mx_kscale(D, 0)[:, None]
    u = mx_kscale(N)
    t = np.random.uniform(0.5, 2.0, N) * u
    v = n((KV, N, 128))
    v[:, :, 127] = 1.0
    return {
        "qT": (n((H, D, NQ)) * s * (0.70 / np.sqrt(D))).astype(np.float32),
        "kT": (n((KV, D, N)) / s).astype(np.float32),
        "t": t.reshape(N, 1).astype(np.float32),
        "v": (v / t[:, None]).astype(np.float32),
        "kb": (0.5 * n((N, 1))).astype(np.float32),
        "mask": (np.arange(N)[:, None] <= np.sort(np.random.randint(N // 4, N, NQ))[None, :]).astype(np.float32),
    }


def reference(qT, kT, t, v, kb, mask):
    a = np.repeat(mxq(f64(kT), 1, "e4m3"), H // KV, 0).transpose(0, 2, 1) @ mxq(f64(qT), 1, "e4m3")
    a = a + f64(kb)
    p = np.exp(a)
    p = p * f64(mask)
    w = p * f64(t)
    y = mxq(w, 1, "e4m3").transpose(0, 2, 1) @ np.repeat(mxq(f64(v), 1, "e4m3"), H // KV, 0)
    y = y / (y[:, :, 127:128])
    return y

@@ -1,0 +1,296 @@
+from contextlib import ExitStack
+
+import concourse.mybir as mybir
+
+H, KV, D, NQ, N = 8, 2, 128, 512, 512
+FLOPS = 2 * 2 * H * NQ * N * D
+
+F32 = mybir.dt.float32
+BF16 = mybir.dt.bfloat16
+U32 = mybir.dt.uint32
+U8 = mybir.dt.uint8
+FP8X4 = mybir.dt.float8_e4m3fn_x4
+ACT = mybir.ActivationFunctionType
+ALU = mybir.AluOpType
+
+P = 128
+PACK = 4
+ROWS = 32
+QB = 128
+SETS = ((0, 1, 4, 5), (2, 3, 6, 7))
+STEPS = [(s, b) for s in range(2) for b in range(NQ // QB)]
+
+
+def tile_rows_kb_mask_gqa_kernel(tc, qT, kT, t, v, kb, mask, out):
+    nc = tc.nc
+    with ExitStack() as ctx:
+        keep = ctx.enter_context(tc.tile_pool(name="keep", bufs=1))
+        work = ctx.enter_context(tc.tile_pool(name="work", bufs=4))
+        psum = ctx.enter_context(tc.psum_pool(name="psum", bufs=1))
+        ctx.enter_context(tc.manual_schedule())
+
+        kb_sb = keep.tile([P, PACK], F32)
+        t_sb = keep.tile([P, PACK], F32)
+        ekb = keep.tile([P, PACK], F32)
+        cvec = keep.tile([P, PACK], F32)
+        k_raw = keep.tile([P, PACK, N], F32)
+        v_raw = keep.tile([P, KV, PACK, D], F32)
+        qa0 = keep.tile([P, PACK, QB], F32)
+        qa1 = keep.tile([P, PACK, NQ - QB], F32)
+        qb_raw = keep.tile([P, PACK, NQ], F32)
+        m0 = keep.tile([P, PACK, QB], F32)
+        m1 = keep.tile([P, PACK, NQ - QB], F32)
+        k_bf = keep.tile([P, PACK, P, PACK], BF16, align_bytes=64)
+        k_codes = keep.tile([P, N], U32, align_bytes=64)
+        k_scales = keep.tile([P, N], U8, align_bytes=64)
+        v_bf = keep.tile([P, KV, D, PACK], BF16, align_bytes=64)
+        v_codes = keep.tile([P, KV * D], U32, align_bytes=64)
+        v_scales = keep.tile([P, KV * D], U8, align_bytes=64)
+        factor = keep.tile([P, NQ // QB, QB, PACK], F32)
+        q_bf = keep.tile([P, len(STEPS), QB, PACK], BF16, align_bytes=64)
+        q_codes = keep.tile([P, len(STEPS), QB], U32, align_bytes=64)
+        q_scales = keep.tile([P, len(STEPS), QB], U8, align_bytes=64)
+        score = [psum.tile([P, PACK, QB], F32, name="score%d" % g) for g in range(4)]
+        ybank = [psum.tile([P, PACK, D], F32, name="ybank%d" % i) for i in range(4)]
+
+        def load_q(eng, dst, s, half, cols):
+            h0 = SETS[s][2 * half]
+            eng.dma_start(
+                out=dst[64 * half : 64 * half + 64],
+                in_=qT[h0 : h0 + 2, :, cols].rearrange("h (p j) n -> (h p) j n", j=PACK),
+            )
+
+        def load_k(eng, g):
+            eng.dma_start(
+                out=k_raw[ROWS * g : ROWS * (g + 1)],
+                in_=kT[g // 2].rearrange("(p j) n -> p j n", j=PACK),
+            )
+
+        first, rest = slice(0, QB), slice(QB, NQ)
+        mask_v = mask.rearrange("(s r) q -> s r q", r=PACK)
+        nc.scalar.dma_start(out=kb_sb[:], in_=kb.rearrange("(s r) o -> s (r o)", r=PACK))
+        nc.sync.dma_start(out=t_sb[:], in_=t.rearrange("(s r) o -> s (r o)", r=PACK))
+        load_q(nc.sync, qa0, 0, 0, first)
+        load_q(nc.scalar, qa0, 0, 1, first)
+        load_k(nc.sync, 0)
+        load_k(nc.scalar, 2)
+        load_k(nc.sync, 1)
+        load_k(nc.scalar, 3)
+        nc.sync.dma_start(out=m0[:], in_=mask_v[:, :, first])
+        nc.sync.dma_start(out=v_raw[:], in_=v.rearrange("k (s j) e -> s k j e", j=PACK))
+        load_q(nc.sync, qa1, 0, 0, rest)
+        load_q(nc.sync, qa1, 0, 1, rest)
+        nc.sync.dma_start(out=m1[:], in_=mask_v[:, :, rest])
+        load_q(nc.sync, qb_raw, 1, 0, slice(0, NQ))
+        load_q(nc.sync, qb_raw, 1, 1, slice(0, NQ))
+
+        def copy(eng, dst, src):
+            if eng == "S":
+                nc.scalar.copy(out=dst, in_=src)
+            else:
+                nc.vector.tensor_copy(out=dst, in_=src)
+
+        def q_src(step):
+            s, b = STEPS[step]
+            if s == 1:
+                return qb_raw[:, :, QB * b : QB * (b + 1)]
+            return qa0[:] if b == 0 else qa1[:, :, QB * (b - 1) : QB * b]
+
+        def q_int(step, eng):
+            copy(
+                eng,
+                q_bf[:, step].rearrange("p (c i) j -> p c j i", i=4),
+                q_src(step).rearrange("p j (c i) -> p c j i", i=4),
+            )
+
+        def q_quant(step):
+            nc.vector.quantize_mx(
+                out=q_codes[:, step, :].bitcast(FP8X4),
+                scales=q_scales[:, step, :],
+                in_=q_bf[:, step].rearrange("p n j -> p (n j)"),
+            )
+
+        def k_int(eng, r0, r1):
+            copy(
+                eng,
+                k_bf[:, r0:r1].rearrange("p r s j -> p s r j"),
+                k_raw[:].rearrange("p j (s r) -> p s r j", r=PACK)[:, :, r0:r1, :],
+            )
+
+        def k_quant(half):
+            cols = slice(256 * half, 256 * (half + 1))
+            nc.vector.quantize_mx(
+                out=k_codes[:, cols].bitcast(FP8X4),
+                scales=k_scales[:, cols],
+                in_=k_bf[:, 2 * half : 2 * half + 2].rearrange("p r s j -> p (r s j)"),
+            )
+
+        def v_int(eng, kv):
+            copy(
+                eng,
+                v_bf[:, kv].rearrange("p (c i) j -> p c j i", i=4),
+                v_raw[:, kv].rearrange("p j (c i) -> p c j i", i=4),
+            )
+
+        def v_quant():
+            nc.vector.quantize_mx(
+                out=v_codes[:].bitcast(FP8X4),
+                scales=v_scales[:],
+                in_=v_bf[:].rearrange("p k e j -> p (k e j)"),
+            )
+
+        def make_factor(b):
+            src = m0[:] if b == 0 else m1[:, :, QB * (b - 1) : QB * b]
+            nc.vector.tensor_tensor(
+                out=factor[:, b],
+                in0=src.rearrange("p r q -> p q r"),
+                in1=cvec[:].unsqueeze(1).to_broadcast([P, QB, PACK]),
+                op=ALU.mult,
+            )
+
+        units = []
+        for step in range(len(STEPS)):
+            if step == 0:
+                groups = [(0,), (1,), (2, 3)]
+            elif step == len(STEPS) - 1:
+                groups = [(0, 1), (2,), (3,)]
+            else:
+                groups = [(0, 1), (2, 3)]
+            units.extend((step, gs) for gs in groups)
+        U = len(units)
+        held = {}
+
+        def scores(u):
+            step, gs = units[u]
+            for g in gs:
+                rows = slice(ROWS * g, ROWS * (g + 1))
+                for r in range(PACK):
+                    cols = slice(P * r, P * (r + 1))
+                    nc.tensor.matmul_mx(
+                        out=score[g][:, r, :],
+                        lhsT=k_codes[rows, cols].bitcast(FP8X4),
+                        lhsT_scale=k_scales[rows, cols],
+                        rhs=q_codes[rows, step, :].bitcast(FP8X4),
+                        rhs_scale=q_scales[rows, step, :],
+                        start=True,
+                        stop=True,
+                    )
+
+        def exps(u):
+            step, gs = units[u]
+            p_t = work.tile([P, len(gs), QB, PACK], F32, tag="p")
+            for i, g in enumerate(gs):
+                nc.scalar.activation(out=p_t[:, i], in_=score[g][:].rearrange("p r q -> p q r"), func=ACT.Exp)
+            held["p", u] = p_t
+
+        def mult(u):
+            step, gs = units[u]
+            w_bf = work.tile([P, len(gs), QB * PACK], BF16, tag="w", align_bytes=64)
+            nc.vector.tensor_tensor(
+                out=w_bf[:],
+                in0=held["p", u][:].rearrange("p g q r -> p g (q r)"),
+                in1=factor[:, STEPS[step][1]].rearrange("p q r -> p (q r)").unsqueeze(1).to_broadcast([P, len(gs), QB * PACK]),
+                op=ALU.mult,
+            )
+            held["w", u] = w_bf
+
+        def quant(u):
+            step, gs = units[u]
+            w_codes = work.tile([P, len(gs) * QB], U32, tag="wc", align_bytes=64)
+            w_scales = work.tile([P, len(gs) * QB], U8, tag="ws", align_bytes=64)
+            nc.vector.quantize_mx(
+                out=w_codes[:].bitcast(FP8X4),
+                scales=w_scales[:],
+                in_=held["w", u][:].rearrange("p g x -> p (g x)"),
+            )
+            held["c", u] = (w_codes, w_scales)
+
+        def values(u):
+            step, gs = units[u]
+            w_codes, w_scales = held["c", u]
+            for i, g in enumerate(gs):
+                cols = slice(QB * i, QB * (i + 1))
+                vc = slice(D * (g // 2), D * (g // 2 + 1))
+                nc.tensor.matmul_mx(
+                    out=ybank[u % 4][:, i, :],
+                    lhsT=w_codes[:, cols].bitcast(FP8X4),
+                    lhsT_scale=w_scales[:, cols],
+                    rhs=v_codes[:, vc].bitcast(FP8X4),
+                    rhs_scale=v_scales[:, vc],
+                    start=True,
+                    stop=True,
+                )
+
+        def recip(u):
+            step, gs = units[u]
+            inv = work.tile([P, len(gs)], F32, tag="inv")
+            nc.vector.reciprocal(out=inv[:], in_=ybank[u % 4][:, 0 : len(gs), D - 1])
+            held["i", u] = inv
+
+        def norm(u, eng):
+            step, gs = units[u]
+            s, b = STEPS[step]
+            inv = held["i", u]
+            res = work.tile([P, len(gs), D], F32, tag="res")
+            if eng == "S":
+                for i in range(len(gs)):
+                    nc.scalar.activation(out=res[:, i, :], in_=ybank[u % 4][:, i, :], func=ACT.Copy, scale=inv[:, i : i + 1])
+            else:
+                nc.vector.tensor_tensor(
+                    out=res[:],
+                    in0=ybank[u % 4][:, 0 : len(gs), :],
+                    in1=inv[:].unsqueeze(2).to_broadcast([P, len(gs), D]),
+                    op=ALU.mult,
+                )
+            h0 = SETS[s][gs[0]]
+            nc.sync.dma_start(
+                out=out[h0 : h0 + len(gs), QB * b : QB * (b + 1), :].rearrange("h q e -> q h e"),
+                in_=res[:],
+            )
+
+        nc.scalar.activation(out=ekb[:], in_=kb_sb[:], func=ACT.Exp)
+        q_int(0, "S")
+        nc.vector.tensor_tensor(out=cvec[:], in0=ekb[:], in1=t_sb[:], op=ALU.mult)
+        q_quant(0)
+        k_int("V", 0, 2)
+        k_int("S", 3, 4)
+        k_int("V", 2, 3)
+        k_quant(0)
+        k_quant(1)
+        make_factor(0)
+        v_int("V", 0)
+        v_int("V", 1)
+        scores(0)
+
+        first_unit = {}
+        for u, (step, gs) in enumerate(units):
+            first_unit.setdefault(step, u)
+        s_extra, v_extra = {}, {}
+        v_extra.setdefault(1, []).append(v_quant)
+        for step in range(1, len(STEPS)):
+            f = first_unit[step]
+            eng = "S" if step in (1, 2, 3, 4, 6) else "V"
+            (s_extra if eng == "S" else v_extra).setdefault(f - 3, []).append(lambda step=step, eng=eng: q_int(step, eng))
+            v_extra.setdefault(f - 2, []).append(lambda step=step: q_quant(step))
+            if step < NQ // QB:
+                v_extra.setdefault(f - 1, []).append(lambda step=step: make_factor(step))
+
+        for k in range(U + 5):
+            if k + 1 < U:
+                scores(k + 1)
+            if k < U:
+                exps(k)
+            for job in s_extra.get(k, []):
+                job()
+            if 0 <= k - 1 < U:
+                mult(k - 1)
+            if 0 <= k - 4 < U:
+                recip(k - 4)
+            if 0 <= k - 2 < U:
+                quant(k - 2)
+            for job in v_extra.get(k, []):
+                job()
+            if 0 <= k - 3 < U:
+                values(k - 3)
+            if 0 <= k - 5 < U:
+                norm(k - 5, "V" if k - 5 == U - 2 else "S")

@@ -1,4 +1,5 @@
 from contextlib import ExitStack
+from functools import partial
 
 import concourse.mybir as mybir
 
@@ -7,6 +8,7 @@ FLOPS = 2 * 2 * H * NQ * N * D
 
 F32 = mybir.dt.float32
 BF16 = mybir.dt.bfloat16
+I32 = mybir.dt.int32
 U32 = mybir.dt.uint32
 U8 = mybir.dt.uint8
 FP8X4 = mybir.dt.float8_e4m3fn_x4
@@ -16,281 +18,336 @@ ALU = mybir.AluOpType
 P = 128
 PACK = 4
 ROWS = 32
+TILES = P // ROWS
 QB = 128
-SETS = ((0, 1, 4, 5), (2, 3, 6, 7))
-STEPS = [(s, b) for s in range(2) for b in range(NQ // QB)]
+BLOCKS = NQ // QB
+STEPS = KV * BLOCKS
+LAST = STEPS - 1
+RUN = 2
+KEY_SPLIT = 96
+ROTATE = 4
+EXP_BUFS = 6
+OUT_BUFS = 8
 
 
 def tile_rows_kb_mask_gqa_kernel(tc, qT, kT, t, v, kb, mask, out):
     nc = tc.nc
     with ExitStack() as ctx:
         keep = ctx.enter_context(tc.tile_pool(name="keep", bufs=1))
-        work = ctx.enter_context(tc.tile_pool(name="work", bufs=4))
+        work = ctx.enter_context(tc.tile_pool(name="work", bufs=ROTATE))
         psum = ctx.enter_context(tc.psum_pool(name="psum", bufs=1))
         ctx.enter_context(tc.manual_schedule())
 
         kb_sb = keep.tile([P, PACK], F32)
         t_sb = keep.tile([P, PACK], F32)
-        ekb = keep.tile([P, PACK], F32)
-        cvec = keep.tile([P, PACK], F32)
-        k_raw = keep.tile([P, PACK, N], F32)
+        exp_kb = keep.tile([P, PACK], F32)
+        token_factor = keep.tile([P, PACK], F32)
+        k_raw = [keep.tile([ROWS, PACK, N], F32, name="k_raw%d" % kv) for kv in range(KV)]
         v_raw = keep.tile([P, KV, PACK, D], F32)
-        qa0 = keep.tile([P, PACK, QB], F32)
-        qa1 = keep.tile([P, PACK, NQ - QB], F32)
-        qb_raw = keep.tile([P, PACK, NQ], F32)
-        m0 = keep.tile([P, PACK, QB], F32)
-        m1 = keep.tile([P, PACK, NQ - QB], F32)
-        k_bf = keep.tile([P, PACK, P, PACK], BF16, align_bytes=64)
-        k_codes = keep.tile([P, N], U32, align_bytes=64)
-        k_scales = keep.tile([P, N], U8, align_bytes=64)
+        q_raw_first = keep.tile([P, PACK, QB], F32)
+        q_raw_rest = keep.tile([P, PACK, NQ - QB], F32)
+        q_raw_second = keep.tile([P, PACK, NQ], F32)
+        mask_0 = keep.tile([P, PACK, QB], F32)
+        mask_1 = keep.tile([P, PACK, QB], F32)
+        mask_23 = keep.tile([P, PACK, 2 * QB], F32)
+        k_bf = [keep.tile([ROWS, PACK, P, PACK], BF16, align_bytes=64, name="k_bf%d" % kv) for kv in range(KV)]
+        k_mx = [keep.tile([P, N + N // PACK], I32, align_bytes=64, name="k_mx%d" % kv) for kv in range(KV)]
         v_bf = keep.tile([P, KV, D, PACK], BF16, align_bytes=64)
         v_codes = keep.tile([P, KV * D], U32, align_bytes=64)
         v_scales = keep.tile([P, KV * D], U8, align_bytes=64)
-        factor = keep.tile([P, NQ // QB, QB, PACK], F32)
-        q_bf = keep.tile([P, len(STEPS), QB, PACK], BF16, align_bytes=64)
-        q_codes = keep.tile([P, len(STEPS), QB], U32, align_bytes=64)
-        q_scales = keep.tile([P, len(STEPS), QB], U8, align_bytes=64)
-        score = [psum.tile([P, PACK, QB], F32, name="score%d" % g) for g in range(4)]
-        ybank = [psum.tile([P, PACK, D], F32, name="ybank%d" % i) for i in range(4)]
+        factor = keep.tile([P, BLOCKS, QB, PACK], F32)
+        q_bf = keep.tile([P, STEPS, QB, PACK], BF16, align_bytes=64)
+        q_codes = keep.tile([P, STEPS, QB], U32, align_bytes=64)
+        q_scales = keep.tile([P, STEPS, QB], U8, align_bytes=64)
+        score_banks = [
+            [psum.tile([P, PACK, QB], F32, name="score%d_%d" % (g, i)) for i in range(2 if g < 2 else 1)]
+            for g in range(TILES)
+        ]
+        y_banks = [psum.tile([P, TILES, D], F32, name="y_bank%d" % i) for i in range(2)]
 
-        def load_q(eng, dst, s, half, cols):
-            h0 = SETS[s][2 * half]
-            eng.dma_start(
-                out=dst[64 * half : 64 * half + 64],
-                in_=qT[h0 : h0 + 2, :, cols].rearrange("h (p j) n -> (h p) j n", j=PACK),
-            )
+        def load(dst, src):
+            nc.sync.dma_start(out=dst[:], in_=src)
 
-        def load_k(eng, g):
-            eng.dma_start(
-                out=k_raw[ROWS * g : ROWS * (g + 1)],
-                in_=kT[g // 2].rearrange("(p j) n -> p j n", j=PACK),
-            )
+        def q_view(kv, cols):
+            return qT[TILES * kv : TILES * (kv + 1), :, cols].rearrange("h (p j) n -> (h p) j n", j=PACK)
 
-        first, rest = slice(0, QB), slice(QB, NQ)
-        mask_v = mask.rearrange("(s r) q -> s r q", r=PACK)
-        nc.scalar.dma_start(out=kb_sb[:], in_=kb.rearrange("(s r) o -> s (r o)", r=PACK))
-        nc.sync.dma_start(out=t_sb[:], in_=t.rearrange("(s r) o -> s (r o)", r=PACK))
-        load_q(nc.sync, qa0, 0, 0, first)
-        load_q(nc.scalar, qa0, 0, 1, first)
-        load_k(nc.sync, 0)
-        load_k(nc.scalar, 2)
-        load_k(nc.sync, 1)
-        load_k(nc.scalar, 3)
-        nc.sync.dma_start(out=m0[:], in_=mask_v[:, :, first])
-        nc.sync.dma_start(out=v_raw[:], in_=v.rearrange("k (s j) e -> s k j e", j=PACK))
-        load_q(nc.sync, qa1, 0, 0, rest)
-        load_q(nc.sync, qa1, 0, 1, rest)
-        nc.sync.dma_start(out=m1[:], in_=mask_v[:, :, rest])
-        load_q(nc.sync, qb_raw, 1, 0, slice(0, NQ))
-        load_q(nc.sync, qb_raw, 1, 1, slice(0, NQ))
+        def k_view(kv):
+            return kT[kv].rearrange("(p j) n -> p j n", j=PACK)
 
-        def copy(eng, dst, src):
-            if eng == "S":
+        mask_view = mask.rearrange("(s r) q -> s r q", r=PACK)
+
+        def interleave(dst, src, on_scalar):
+            if on_scalar:
                 nc.scalar.copy(out=dst, in_=src)
             else:
                 nc.vector.tensor_copy(out=dst, in_=src)
 
-        def q_src(step):
-            s, b = STEPS[step]
-            if s == 1:
-                return qb_raw[:, :, QB * b : QB * (b + 1)]
-            return qa0[:] if b == 0 else qa1[:, :, QB * (b - 1) : QB * b]
+        def quantize(codes, scales, src):
+            nc.vector.quantize_mx(out=codes.bitcast(FP8X4), scales=scales, in_=src)
 
-        def q_int(step, eng):
-            copy(
-                eng,
-                q_bf[:, step].rearrange("p (c i) j -> p c j i", i=4),
-                q_src(step).rearrange("p j (c i) -> p c j i", i=4),
+        def interleave_q(step, on_scalar):
+            kv, b = divmod(step, BLOCKS)
+            if kv == 1:
+                src = q_raw_second[:, :, QB * b : QB * (b + 1)]
+            elif b == 0:
+                src = q_raw_first[:]
+            else:
+                src = q_raw_rest[:, :, QB * (b - 1) : QB * b]
+            interleave(
+                q_bf[:, step].rearrange("p (c i) j -> p c j i", i=RUN),
+                src.rearrange("p j (c i) -> p c j i", i=RUN),
+                on_scalar,
             )
 
-        def q_quant(step):
-            nc.vector.quantize_mx(
-                out=q_codes[:, step, :].bitcast(FP8X4),
-                scales=q_scales[:, step, :],
-                in_=q_bf[:, step].rearrange("p n j -> p (n j)"),
+        def quantize_q(step):
+            quantize(q_codes[:, step, :], q_scales[:, step, :], q_bf[:, step].rearrange("p n j -> p (n j)"))
+
+        def interleave_k(kv, s0, s1, on_scalar):
+            interleave(
+                k_bf[kv][:].rearrange("p r s j -> p s r j")[:, s0:s1],
+                k_raw[kv][:].rearrange("p j (s r) -> p s r j", r=PACK)[:, s0:s1],
+                on_scalar,
             )
 
-        def k_int(eng, r0, r1):
-            copy(
-                eng,
-                k_bf[:, r0:r1].rearrange("p r s j -> p s r j"),
-                k_raw[:].rearrange("p j (s r) -> p s r j", r=PACK)[:, :, r0:r1, :],
+        def quantize_k(kv):
+            quantize(
+                k_mx[kv][:ROWS, :N],
+                k_mx[kv][:ROWS, N:].bitcast(U8),
+                k_bf[kv][:].rearrange("p r s j -> p (r s j)"),
+            )
+            for g in range(1, TILES):
+                nc.sync.dma_start(out=k_mx[kv][ROWS * g : ROWS * (g + 1), :], in_=k_mx[kv][:ROWS, :])
+
+        def interleave_v(kv, on_scalar):
+            interleave(
+                v_bf[:, kv].rearrange("p (c i) j -> p c j i", i=RUN),
+                v_raw[:, kv].rearrange("p j (c i) -> p c j i", i=RUN),
+                on_scalar,
             )
 
-        def k_quant(half):
-            cols = slice(256 * half, 256 * (half + 1))
-            nc.vector.quantize_mx(
-                out=k_codes[:, cols].bitcast(FP8X4),
-                scales=k_scales[:, cols],
-                in_=k_bf[:, 2 * half : 2 * half + 2].rearrange("p r s j -> p (r s j)"),
-            )
-
-        def v_int(eng, kv):
-            copy(
-                eng,
-                v_bf[:, kv].rearrange("p (c i) j -> p c j i", i=4),
-                v_raw[:, kv].rearrange("p j (c i) -> p c j i", i=4),
-            )
-
-        def v_quant():
-            nc.vector.quantize_mx(
-                out=v_codes[:].bitcast(FP8X4),
-                scales=v_scales[:],
-                in_=v_bf[:].rearrange("p k e j -> p (k e j)"),
-            )
+        def quantize_v():
+            quantize(v_codes[:], v_scales[:], v_bf[:].rearrange("p k e j -> p (k e j)"))
 
         def make_factor(b):
-            src = m0[:] if b == 0 else m1[:, :, QB * (b - 1) : QB * b]
+            src = (mask_0[:], mask_1[:], mask_23[:, :, :QB], mask_23[:, :, QB:])[b]
             nc.vector.tensor_tensor(
-                out=factor[:, b],
-                in0=src.rearrange("p r q -> p q r"),
-                in1=cvec[:].unsqueeze(1).to_broadcast([P, QB, PACK]),
+                out=factor[:, b].rearrange("p (c i) r -> p c r i", i=RUN),
+                in0=src.rearrange("p r (c i) -> p c r i", i=RUN),
+                in1=token_factor[:].unsqueeze(1).unsqueeze(3).to_broadcast([P, QB // RUN, PACK, RUN]),
                 op=ALU.mult,
             )
 
-        units = []
-        for step in range(len(STEPS)):
-            if step == 0:
-                groups = [(0,), (1,), (2, 3)]
-            elif step == len(STEPS) - 1:
-                groups = [(0, 1), (2,), (3,)]
-            else:
-                groups = [(0, 1), (2, 3)]
-            units.extend((step, gs) for gs in groups)
-        U = len(units)
-        held = {}
+        exp_tiles, w_tiles, w_mx, inverses = {}, {}, {}, {}
 
-        def scores(u):
-            step, gs = units[u]
-            for g in gs:
-                rows = slice(ROWS * g, ROWS * (g + 1))
-                for r in range(PACK):
-                    cols = slice(P * r, P * (r + 1))
+        def score_bank(step, g):
+            return score_banks[g][step % len(score_banks[g])]
+
+        def scores(step, tiles):
+            keys = k_mx[step // BLOCKS]
+            for r in range(PACK):
+                cols = slice(P * r, P * (r + 1))
+                for g in tiles:
+                    rows = slice(ROWS * g, ROWS * (g + 1))
                     nc.tensor.matmul_mx(
-                        out=score[g][:, r, :],
-                        lhsT=k_codes[rows, cols].bitcast(FP8X4),
-                        lhsT_scale=k_scales[rows, cols],
+                        out=score_bank(step, g)[:, r, :],
+                        lhsT=keys[rows, cols].bitcast(FP8X4),
+                        lhsT_scale=keys[rows, N:].bitcast(U8)[:, cols],
                         rhs=q_codes[rows, step, :].bitcast(FP8X4),
                         rhs_scale=q_scales[rows, step, :],
                         start=True,
                         stop=True,
                     )
 
-        def exps(u):
-            step, gs = units[u]
-            p_t = work.tile([P, len(gs), QB, PACK], F32, tag="p")
-            for i, g in enumerate(gs):
-                nc.scalar.activation(out=p_t[:, i], in_=score[g][:].rearrange("p r q -> p q r"), func=ACT.Exp)
-            held["p", u] = p_t
+        def exponential(step, g):
+            pair, i = divmod(g, 2)
+            if i == 0:
+                exp_tiles[step, pair] = work.tile([P, 2, QB, PACK], F32, name="exp_a", bufs=EXP_BUFS)
+            nc.scalar.activation(
+                out=exp_tiles[step, pair][:, i],
+                in_=score_bank(step, g)[:].rearrange("p r q -> p q r"),
+                func=ACT.Exp,
+            )
 
-        def mult(u):
-            step, gs = units[u]
-            w_bf = work.tile([P, len(gs), QB * PACK], BF16, tag="w", align_bytes=64)
+        def weigh(step, pair, lo=0, hi=2):
+            if lo == 0:
+                w_tiles[step, pair] = work.tile([P, 2, QB * PACK], BF16, name="w", align_bytes=64)
+            shared = factor[:, step % BLOCKS].rearrange("p q r -> p (q r)")
             nc.vector.tensor_tensor(
-                out=w_bf[:],
-                in0=held["p", u][:].rearrange("p g q r -> p g (q r)"),
-                in1=factor[:, STEPS[step][1]].rearrange("p q r -> p (q r)").unsqueeze(1).to_broadcast([P, len(gs), QB * PACK]),
+                out=w_tiles[step, pair][:, lo:hi],
+                in0=exp_tiles[step, pair][:, lo:hi].rearrange("p g q r -> p g (q r)"),
+                in1=shared.unsqueeze(1).to_broadcast([P, hi - lo, QB * PACK]),
                 op=ALU.mult,
             )
-            held["w", u] = w_bf
 
-        def quant(u):
-            step, gs = units[u]
-            w_codes = work.tile([P, len(gs) * QB], U32, tag="wc", align_bytes=64)
-            w_scales = work.tile([P, len(gs) * QB], U8, tag="ws", align_bytes=64)
-            nc.vector.quantize_mx(
-                out=w_codes[:].bitcast(FP8X4),
-                scales=w_scales[:],
-                in_=held["w", u][:].rearrange("p g x -> p (g x)"),
-            )
-            held["c", u] = (w_codes, w_scales)
+        def quantize_w(step, pair, lo=0, hi=2):
+            if lo == 0:
+                w_codes = work.tile([P, 2 * QB], U32, align_bytes=64)
+                w_scales = work.tile([P, 2 * QB], U8, align_bytes=64)
+                w_mx[step, pair] = (w_codes, w_scales)
+            w_codes, w_scales = w_mx[step, pair]
+            cols = slice(QB * lo, QB * hi)
+            quantize(w_codes[:, cols], w_scales[:, cols], w_tiles[step, pair][:, lo:hi].rearrange("p g x -> p (g x)"))
 
-        def values(u):
-            step, gs = units[u]
-            w_codes, w_scales = held["c", u]
-            for i, g in enumerate(gs):
+        def y_places(pair):
+            return slice(2 * (1 - pair), 2 * (2 - pair))
+
+        def y_pair(step, pair):
+            return y_banks[(step + pair) % 2][:, y_places(pair), :]
+
+        def values(step, pair, lo=0, hi=2):
+            w_codes, w_scales = w_mx[step, pair]
+            kv = step // BLOCKS
+            v_cols = slice(D * kv, D * (kv + 1))
+            for i in range(lo, hi):
                 cols = slice(QB * i, QB * (i + 1))
-                vc = slice(D * (g // 2), D * (g // 2 + 1))
                 nc.tensor.matmul_mx(
-                    out=ybank[u % 4][:, i, :],
+                    out=y_pair(step, pair)[:, i, :],
                     lhsT=w_codes[:, cols].bitcast(FP8X4),
                     lhsT_scale=w_scales[:, cols],
-                    rhs=v_codes[:, vc].bitcast(FP8X4),
-                    rhs_scale=v_scales[:, vc],
+                    rhs=v_codes[:, v_cols].bitcast(FP8X4),
+                    rhs_scale=v_scales[:, v_cols],
                     start=True,
                     stop=True,
                 )
 
-        def recip(u):
-            step, gs = units[u]
-            inv = work.tile([P, len(gs)], F32, tag="inv")
-            nc.vector.reciprocal(out=inv[:], in_=ybank[u % 4][:, 0 : len(gs), D - 1])
-            held["i", u] = inv
+        def invert(group):
+            lo = 2 if group == 0 else 0
+            hi = 2 if group == STEPS else TILES
+            inverse = work.tile([P, TILES], F32)
+            nc.vector.reciprocal(out=inverse[:, lo:hi], in_=y_banks[group % 2][:, lo:hi, D - 1])
+            inverses[group] = inverse
 
-        def norm(u, eng):
-            step, gs = units[u]
-            s, b = STEPS[step]
-            inv = held["i", u]
-            res = work.tile([P, len(gs), D], F32, tag="res")
-            if eng == "S":
-                for i in range(len(gs)):
-                    nc.scalar.activation(out=res[:, i, :], in_=ybank[u % 4][:, i, :], func=ACT.Copy, scale=inv[:, i : i + 1])
-            else:
-                nc.vector.tensor_tensor(
-                    out=res[:],
-                    in0=ybank[u % 4][:, 0 : len(gs), :],
-                    in1=inv[:].unsqueeze(2).to_broadcast([P, len(gs), D]),
-                    op=ALU.mult,
+        def out_view(step, pair):
+            kv, b = divmod(step, BLOCKS)
+            head = TILES * kv + 2 * pair
+            return out[head : head + 2, QB * b : QB * (b + 1), :].rearrange("h q e -> q h e")
+
+        def divide(step, pair):
+            inverse = inverses[step + pair][:, y_places(pair)]
+            result = work.tile([P, 2, D], F32, name="result", bufs=OUT_BUFS)
+            for i in range(2):
+                nc.scalar.activation(
+                    out=result[:, i, :], in_=y_pair(step, pair)[:, i, :], func=ACT.Copy, scale=inverse[:, i : i + 1]
                 )
-            h0 = SETS[s][gs[0]]
-            nc.sync.dma_start(
-                out=out[h0 : h0 + len(gs), QB * b : QB * (b + 1), :].rearrange("h q e -> q h e"),
-                in_=res[:],
+            nc.sync.dma_start(out=out_view(step, pair), in_=result[:])
+
+        def divide_last_pair():
+            inverse = inverses[STEPS][:, y_places(1)]
+            result = work.tile([P, 2, D], F32, name="result", bufs=OUT_BUFS)
+            nc.vector.tensor_tensor(
+                out=result[:], in0=y_pair(LAST, 1), in1=inverse.unsqueeze(2).to_broadcast([P, 2, D]), op=ALU.mult
             )
+            for i, queue in enumerate((nc.sync, nc.scalar)):
+                queue.dma_start(out=out_view(LAST, 1)[:, i, :], in_=result[:, i, :])
 
-        nc.scalar.activation(out=ekb[:], in_=kb_sb[:], func=ACT.Exp)
-        q_int(0, "S")
-        nc.vector.tensor_tensor(out=cvec[:], in0=ekb[:], in1=t_sb[:], op=ALU.mult)
-        q_quant(0)
-        k_int("V", 0, 2)
-        k_int("S", 3, 4)
-        k_int("V", 2, 3)
-        k_quant(0)
-        k_quant(1)
+        nc.scalar.dma_start(out=kb_sb[:], in_=kb.rearrange("(s r) o -> s (r o)", r=PACK))
+        nc.scalar.dma_start(out=t_sb[:], in_=t.rearrange("(s r) o -> s (r o)", r=PACK))
+        load(k_raw[0], k_view(0))
+        load(q_raw_first, q_view(0, slice(0, QB)))
+        load(q_raw_rest, q_view(0, slice(QB, NQ)))
+        load(mask_0, mask_view[:, :, :QB])
+        for kv in range(KV):
+            nc.vector.memset(k_mx[kv][:ROWS, N:], 0)
+        nc.scalar.activation(out=exp_kb[:], in_=kb_sb[:], func=ACT.Exp)
+        interleave_k(0, 0, KEY_SPLIT, False)
+        interleave_k(0, KEY_SPLIT, P, True)
+        interleave_q(0, True)
+        quantize_k(0)
+        load(mask_1, mask_view[:, :, QB : 2 * QB])
+        load(k_raw[1], k_view(1))
+        load(v_raw, v.rearrange("k (s j) e -> s k j e", j=PACK))
+        load(mask_23, mask_view[:, :, 2 * QB :])
+        load(q_raw_second, q_view(1, slice(0, NQ)))
+        quantize_q(0)
+        nc.vector.tensor_tensor(out=token_factor[:], in0=exp_kb[:], in1=t_sb[:], op=ALU.mult)
+        scores(0, (0,))
+        scores(0, (1,))
+        scores(0, (2, 3))
         make_factor(0)
-        v_int("V", 0)
-        v_int("V", 1)
-        scores(0)
+        interleave_q(1, False)
+        quantize_q(1)
+        scores(1, (0, 1))
 
-        first_unit = {}
-        for u, (step, gs) in enumerate(units):
-            first_unit.setdefault(step, u)
-        s_extra, v_extra = {}, {}
-        v_extra.setdefault(1, []).append(v_quant)
-        for step in range(1, len(STEPS)):
-            f = first_unit[step]
-            eng = "S" if step in (1, 2, 3, 4, 6) else "V"
-            (s_extra if eng == "S" else v_extra).setdefault(f - 3, []).append(lambda step=step, eng=eng: q_int(step, eng))
-            v_extra.setdefault(f - 2, []).append(lambda step=step: q_quant(step))
-            if step < NQ // QB:
-                v_extra.setdefault(f - 1, []).append(lambda step=step: make_factor(step))
+        half = P // 2
+        jobs = {
+            (0, "exp 0"): [
+                partial(interleave_q, 2, True),
+                partial(interleave_q, 3, True),
+                partial(make_factor, 1),
+                partial(quantize_q, 2),
+                partial(quantize_q, 3),
+            ],
+            (0, "weigh 0"): [partial(interleave_k, 1, half, P, False)],
+            (1, "exp 1"): [partial(interleave_v, 1, True)],
+            (1, "weigh 0"): [partial(interleave_v, 0, False), partial(make_factor, 2)],
+            (1, "exp 3"): [partial(interleave_k, 1, 0, half, True)],
+            (1, "weigh 1"): [quantize_v],
+            (1, "quantize 0"): [partial(quantize_k, 1), partial(values, 0, 0)],
+            (2, "exp 0"): [partial(interleave_q, 4, True)],
+            (2, "weigh 0"): [partial(invert, 0)],
+            (2, "invert"): [partial(make_factor, 3)],
+            (2, "exp 2"): [partial(interleave_q, 5, True), partial(interleave_q, 6, True)],
+            (3, "exp 2"): [partial(interleave_q, 7, True)],
+        }
 
-        for k in range(U + 5):
-            if k + 1 < U:
-                scores(k + 1)
-            if k < U:
-                exps(k)
-            for job in s_extra.get(k, []):
+        def after(step, stage):
+            for job in jobs.get((step, stage), []):
                 job()
-            if 0 <= k - 1 < U:
-                mult(k - 1)
-            if 0 <= k - 4 < U:
-                recip(k - 4)
-            if 0 <= k - 2 < U:
-                quant(k - 2)
-            for job in v_extra.get(k, []):
-                job()
-            if 0 <= k - 3 < U:
-                values(k - 3)
-            if 0 <= k - 5 < U:
-                norm(k - 5, "V" if k - 5 == U - 2 else "S")
+
+        def first_three_heads(step):
+            exponential(step, 0)
+            if step == 0:
+                weigh(step, 0, 0, 1)
+            after(step, "exp 0")
+            exponential(step, 1)
+            after(step, "exp 1")
+            if step >= 3:
+                divide(step - 3, 1)
+            weigh(step, 0, 1 if step == 0 else 0, 2)
+            after(step, "weigh 0")
+            if step >= 1:
+                quantize_w(step - 1, 1)
+            if step >= 2:
+                invert(step - 1)
+            after(step, "invert")
+            if BLOCKS <= step + 2 <= LAST:
+                quantize_q(step + 2)
+            exponential(step, 2)
+            after(step, "exp 2")
+
+        for step in range(LAST):
+            first_three_heads(step)
+            exponential(step, 3)
+            after(step, "exp 3")
+            if step >= 2:
+                divide(step - 2, 0)
+            scores(step + 1, (2, 3))
+            if step + 2 <= LAST:
+                scores(step + 2, (0, 1))
+            weigh(step, 1)
+            after(step, "weigh 1")
+            quantize_w(step, 0)
+            after(step, "quantize 0")
+            if step >= 1:
+                values(step - 1, 1)
+                values(step, 0)
+
+        first_three_heads(LAST)
+        divide(LAST - 2, 0)
+        weigh(LAST, 1, 0, 1)
+        exponential(LAST, 3)
+        quantize_w(LAST, 0)
+        values(LAST - 1, 1)
+        values(LAST, 0)
+        divide(LAST - 2, 1)
+        divide(LAST - 1, 0)
+        weigh(LAST, 1, 1, 2)
+        quantize_w(LAST, 1, 0, 1)
+        values(LAST, 1, 0, 1)
+        invert(LAST)
+        quantize_w(LAST, 1, 1, 2)
+        values(LAST, 1, 1, 2)
+        divide(LAST - 1, 1)
+        divide(LAST, 0)
+        invert(STEPS)
+        divide_last_pair()

from contextlib import ExitStack
from functools import partial

import concourse.mybir as mybir

H, KV, D, NQ, N = 8, 2, 128, 512, 512
FLOPS = 2 * 2 * H * NQ * N * D

F32 = mybir.dt.float32
BF16 = mybir.dt.bfloat16
I32 = mybir.dt.int32
U32 = mybir.dt.uint32
U8 = mybir.dt.uint8
FP8X4 = mybir.dt.float8_e4m3fn_x4
ACT = mybir.ActivationFunctionType
ALU = mybir.AluOpType

P = 128
PACK = 4
ROWS = 32
TILES = P // ROWS
QB = 128
BLOCKS = NQ // QB
STEPS = KV * BLOCKS
LAST = STEPS - 1
RUN = 2
KEY_SPLIT = 96
ROTATE = 4
EXP_BUFS = 6
OUT_BUFS = 8


def tile_rows_kb_mask_gqa_kernel(tc, qT, kT, t, v, kb, mask, out):
    nc = tc.nc
    with ExitStack() as ctx:
        keep = ctx.enter_context(tc.tile_pool(name="keep", bufs=1))
        work = ctx.enter_context(tc.tile_pool(name="work", bufs=ROTATE))
        psum = ctx.enter_context(tc.psum_pool(name="psum", bufs=1))
        ctx.enter_context(tc.manual_schedule())

        kb_sb = keep.tile([P, PACK], F32)
        t_sb = keep.tile([P, PACK], F32)
        exp_kb = keep.tile([P, PACK], F32)
        token_factor = keep.tile([P, PACK], F32)
        k_raw = [keep.tile([ROWS, PACK, N], F32, name="k_raw%d" % kv) for kv in range(KV)]
        v_raw = keep.tile([P, KV, PACK, D], F32)
        q_raw_first = keep.tile([P, PACK, QB], F32)
        q_raw_rest = keep.tile([P, PACK, NQ - QB], F32)
        q_raw_second = keep.tile([P, PACK, NQ], F32)
        mask_0 = keep.tile([P, PACK, QB], F32)
        mask_1 = keep.tile([P, PACK, QB], F32)
        mask_23 = keep.tile([P, PACK, 2 * QB], F32)
        k_bf = [keep.tile([ROWS, PACK, P, PACK], BF16, align_bytes=64, name="k_bf%d" % kv) for kv in range(KV)]
        k_mx = [keep.tile([P, N + N // PACK], I32, align_bytes=64, name="k_mx%d" % kv) for kv in range(KV)]
        v_bf = keep.tile([P, KV, D, PACK], BF16, align_bytes=64)
        v_codes = keep.tile([P, KV * D], U32, align_bytes=64)
        v_scales = keep.tile([P, KV * D], U8, align_bytes=64)
        factor = keep.tile([P, BLOCKS, QB, PACK], F32)
        q_bf = keep.tile([P, STEPS, QB, PACK], BF16, align_bytes=64)
        q_codes = keep.tile([P, STEPS, QB], U32, align_bytes=64)
        q_scales = keep.tile([P, STEPS, QB], U8, align_bytes=64)
        score_banks = [
            [psum.tile([P, PACK, QB], F32, name="score%d_%d" % (g, i)) for i in range(2 if g < 2 else 1)]
            for g in range(TILES)
        ]
        y_banks = [psum.tile([P, TILES, D], F32, name="y_bank%d" % i) for i in range(2)]

        def load(dst, src):
            nc.sync.dma_start(out=dst[:], in_=src)

        def q_view(kv, cols):
            return qT[TILES * kv : TILES * (kv + 1), :, cols].rearrange("h (p j) n -> (h p) j n", j=PACK)

        def k_view(kv):
            return kT[kv].rearrange("(p j) n -> p j n", j=PACK)

        mask_view = mask.rearrange("(s r) q -> s r q", r=PACK)

        def interleave(dst, src, on_scalar):
            if on_scalar:
                nc.scalar.copy(out=dst, in_=src)
            else:
                nc.vector.tensor_copy(out=dst, in_=src)

        def quantize(codes, scales, src):
            nc.vector.quantize_mx(out=codes.bitcast(FP8X4), scales=scales, in_=src)

        def interleave_q(step, on_scalar):
            kv, b = divmod(step, BLOCKS)
            if kv == 1:
                src = q_raw_second[:, :, QB * b : QB * (b + 1)]
            elif b == 0:
                src = q_raw_first[:]
            else:
                src = q_raw_rest[:, :, QB * (b - 1) : QB * b]
            interleave(
                q_bf[:, step].rearrange("p (c i) j -> p c j i", i=RUN),
                src.rearrange("p j (c i) -> p c j i", i=RUN),
                on_scalar,
            )

        def quantize_q(step):
            quantize(q_codes[:, step, :], q_scales[:, step, :], q_bf[:, step].rearrange("p n j -> p (n j)"))

        def interleave_k(kv, s0, s1, on_scalar):
            interleave(
                k_bf[kv][:].rearrange("p r s j -> p s r j")[:, s0:s1],
                k_raw[kv][:].rearrange("p j (s r) -> p s r j", r=PACK)[:, s0:s1],
                on_scalar,
            )

        def quantize_k(kv):
            quantize(
                k_mx[kv][:ROWS, :N],
                k_mx[kv][:ROWS, N:].bitcast(U8),
                k_bf[kv][:].rearrange("p r s j -> p (r s j)"),
            )
            for g in range(1, TILES):
                nc.sync.dma_start(out=k_mx[kv][ROWS * g : ROWS * (g + 1), :], in_=k_mx[kv][:ROWS, :])

        def interleave_v(kv, on_scalar):
            interleave(
                v_bf[:, kv].rearrange("p (c i) j -> p c j i", i=RUN),
                v_raw[:, kv].rearrange("p j (c i) -> p c j i", i=RUN),
                on_scalar,
            )

        def quantize_v():
            quantize(v_codes[:], v_scales[:], v_bf[:].rearrange("p k e j -> p (k e j)"))

        def make_factor(b):
            src = (mask_0[:], mask_1[:], mask_23[:, :, :QB], mask_23[:, :, QB:])[b]
            nc.vector.tensor_tensor(
                out=factor[:, b].rearrange("p (c i) r -> p c r i", i=RUN),
                in0=src.rearrange("p r (c i) -> p c r i", i=RUN),
                in1=token_factor[:].unsqueeze(1).unsqueeze(3).to_broadcast([P, QB // RUN, PACK, RUN]),
                op=ALU.mult,
            )

        exp_tiles, w_tiles, w_mx, inverses = {}, {}, {}, {}

        def score_bank(step, g):
            return score_banks[g][step % len(score_banks[g])]

        def scores(step, tiles):
            keys = k_mx[step // BLOCKS]
            for r in range(PACK):
                cols = slice(P * r, P * (r + 1))
                for g in tiles:
                    rows = slice(ROWS * g, ROWS * (g + 1))
                    nc.tensor.matmul_mx(
                        out=score_bank(step, g)[:, r, :],
                        lhsT=keys[rows, cols].bitcast(FP8X4),
                        lhsT_scale=keys[rows, N:].bitcast(U8)[:, cols],
                        rhs=q_codes[rows, step, :].bitcast(FP8X4),
                        rhs_scale=q_scales[rows, step, :],
                        start=True,
                        stop=True,
                    )

        def exponential(step, g):
            pair, i = divmod(g, 2)
            if i == 0:
                exp_tiles[step, pair] = work.tile([P, 2, QB, PACK], F32, name="exp_a", bufs=EXP_BUFS)
            nc.scalar.activation(
                out=exp_tiles[step, pair][:, i],
                in_=score_bank(step, g)[:].rearrange("p r q -> p q r"),
                func=ACT.Exp,
            )

        def weigh(step, pair, lo=0, hi=2):
            if lo == 0:
                w_tiles[step, pair] = work.tile([P, 2, QB * PACK], BF16, name="w", align_bytes=64)
            shared = factor[:, step % BLOCKS].rearrange("p q r -> p (q r)")
            nc.vector.tensor_tensor(
                out=w_tiles[step, pair][:, lo:hi],
                in0=exp_tiles[step, pair][:, lo:hi].rearrange("p g q r -> p g (q r)"),
                in1=shared.unsqueeze(1).to_broadcast([P, hi - lo, QB * PACK]),
                op=ALU.mult,
            )

        def quantize_w(step, pair, lo=0, hi=2):
            if lo == 0:
                w_codes = work.tile([P, 2 * QB], U32, align_bytes=64)
                w_scales = work.tile([P, 2 * QB], U8, align_bytes=64)
                w_mx[step, pair] = (w_codes, w_scales)
            w_codes, w_scales = w_mx[step, pair]
            cols = slice(QB * lo, QB * hi)
            quantize(w_codes[:, cols], w_scales[:, cols], w_tiles[step, pair][:, lo:hi].rearrange("p g x -> p (g x)"))

        def y_places(pair):
            return slice(2 * (1 - pair), 2 * (2 - pair))

        def y_pair(step, pair):
            return y_banks[(step + pair) % 2][:, y_places(pair), :]

        def values(step, pair, lo=0, hi=2):
            w_codes, w_scales = w_mx[step, pair]
            kv = step // BLOCKS
            v_cols = slice(D * kv, D * (kv + 1))
            for i in range(lo, hi):
                cols = slice(QB * i, QB * (i + 1))
                nc.tensor.matmul_mx(
                    out=y_pair(step, pair)[:, i, :],
                    lhsT=w_codes[:, cols].bitcast(FP8X4),
                    lhsT_scale=w_scales[:, cols],
                    rhs=v_codes[:, v_cols].bitcast(FP8X4),
                    rhs_scale=v_scales[:, v_cols],
                    start=True,
                    stop=True,
                )

        def invert(group):
            lo = 2 if group == 0 else 0
            hi = 2 if group == STEPS else TILES
            inverse = work.tile([P, TILES], F32)
            nc.vector.reciprocal(out=inverse[:, lo:hi], in_=y_banks[group % 2][:, lo:hi, D - 1])
            inverses[group] = inverse

        def out_view(step, pair):
            kv, b = divmod(step, BLOCKS)
            head = TILES * kv + 2 * pair
            return out[head : head + 2, QB * b : QB * (b + 1), :].rearrange("h q e -> q h e")

        def divide(step, pair):
            inverse = inverses[step + pair][:, y_places(pair)]
            result = work.tile([P, 2, D], F32, name="result", bufs=OUT_BUFS)
            for i in range(2):
                nc.scalar.activation(
                    out=result[:, i, :], in_=y_pair(step, pair)[:, i, :], func=ACT.Copy, scale=inverse[:, i : i + 1]
                )
            nc.sync.dma_start(out=out_view(step, pair), in_=result[:])

        def divide_last_pair():
            inverse = inverses[STEPS][:, y_places(1)]
            result = work.tile([P, 2, D], F32, name="result", bufs=OUT_BUFS)
            nc.vector.tensor_tensor(
                out=result[:], in0=y_pair(LAST, 1), in1=inverse.unsqueeze(2).to_broadcast([P, 2, D]), op=ALU.mult
            )
            for i, queue in enumerate((nc.sync, nc.scalar)):
                queue.dma_start(out=out_view(LAST, 1)[:, i, :], in_=result[:, i, :])

        nc.scalar.dma_start(out=kb_sb[:], in_=kb.rearrange("(s r) o -> s (r o)", r=PACK))
        nc.scalar.dma_start(out=t_sb[:], in_=t.rearrange("(s r) o -> s (r o)", r=PACK))
        load(k_raw[0], k_view(0))
        load(q_raw_first, q_view(0, slice(0, QB)))
        load(q_raw_rest, q_view(0, slice(QB, NQ)))
        load(mask_0, mask_view[:, :, :QB])
        for kv in range(KV):
            nc.vector.memset(k_mx[kv][:ROWS, N:], 0)
        nc.scalar.activation(out=exp_kb[:], in_=kb_sb[:], func=ACT.Exp)
        interleave_k(0, 0, KEY_SPLIT, False)
        interleave_k(0, KEY_SPLIT, P, True)
        interleave_q(0, True)
        quantize_k(0)
        load(mask_1, mask_view[:, :, QB : 2 * QB])
        load(k_raw[1], k_view(1))
        load(v_raw, v.rearrange("k (s j) e -> s k j e", j=PACK))
        load(mask_23, mask_view[:, :, 2 * QB :])
        load(q_raw_second, q_view(1, slice(0, NQ)))
        quantize_q(0)
        nc.vector.tensor_tensor(out=token_factor[:], in0=exp_kb[:], in1=t_sb[:], op=ALU.mult)
        scores(0, (0,))
        scores(0, (1,))
        scores(0, (2, 3))
        make_factor(0)
        interleave_q(1, False)
        quantize_q(1)
        scores(1, (0, 1))

        half = P // 2
        jobs = {
            (0, "exp 0"): [
                partial(interleave_q, 2, True),
                partial(interleave_q, 3, True),
                partial(make_factor, 1),
                partial(quantize_q, 2),
                partial(quantize_q, 3),
            ],
            (0, "weigh 0"): [partial(interleave_k, 1, half, P, False)],
            (1, "exp 1"): [partial(interleave_v, 1, True)],
            (1, "weigh 0"): [partial(interleave_v, 0, False), partial(make_factor, 2)],
            (1, "exp 3"): [partial(interleave_k, 1, 0, half, True)],
            (1, "weigh 1"): [quantize_v],
            (1, "quantize 0"): [partial(quantize_k, 1), partial(values, 0, 0)],
            (2, "exp 0"): [partial(interleave_q, 4, True)],
            (2, "weigh 0"): [partial(invert, 0)],
            (2, "invert"): [partial(make_factor, 3)],
            (2, "exp 2"): [partial(interleave_q, 5, True), partial(interleave_q, 6, True)],
            (3, "exp 2"): [partial(interleave_q, 7, True)],
        }

        def after(step, stage):
            for job in jobs.get((step, stage), []):
                job()

        def first_three_heads(step):
            exponential(step, 0)
            if step == 0:
                weigh(step, 0, 0, 1)
            after(step, "exp 0")
            exponential(step, 1)
            after(step, "exp 1")
            if step >= 3:
                divide(step - 3, 1)
            weigh(step, 0, 1 if step == 0 else 0, 2)
            after(step, "weigh 0")
            if step >= 1:
                quantize_w(step - 1, 1)
            if step >= 2:
                invert(step - 1)
            after(step, "invert")
            if BLOCKS <= step + 2 <= LAST:
                quantize_q(step + 2)
            exponential(step, 2)
            after(step, "exp 2")

        for step in range(LAST):
            first_three_heads(step)
            exponential(step, 3)
            after(step, "exp 3")
            if step >= 2:
                divide(step - 2, 0)
            scores(step + 1, (2, 3))
            if step + 2 <= LAST:
                scores(step + 2, (0, 1))
            weigh(step, 1)
            after(step, "weigh 1")
            quantize_w(step, 0)
            after(step, "quantize 0")
            if step >= 1:
                values(step - 1, 1)
                values(step, 0)

        first_three_heads(LAST)
        divide(LAST - 2, 0)
        weigh(LAST, 1, 0, 1)
        exponential(LAST, 3)
        quantize_w(LAST, 0)
        values(LAST - 1, 1)
        values(LAST, 0)
        divide(LAST - 2, 1)
        divide(LAST - 1, 0)
        weigh(LAST, 1, 1, 2)
        quantize_w(LAST, 1, 0, 1)
        values(LAST, 1, 0, 1)
        invert(LAST)
        quantize_w(LAST, 1, 1, 2)
        values(LAST, 1, 1, 2)
        divide(LAST - 1, 1)
        divide(LAST, 0)
        invert(STEPS)
        divide_last_pair()
